import numpy as np
import ml_dtypes


def mxq(x, axis, fmt="e4m3"):
    dtype, down = {"e4m3": (ml_dtypes.float8_e4m3fn, 7), "e5m2": (ml_dtypes.float8_e5m2, 14)}[fmt]
    v = np.moveaxis(np.asarray(x, np.float32).astype(ml_dtypes.bfloat16).astype(np.float64), axis, -1)
    blocks = v.reshape(v.shape[:-1] + (-1, 32))
    amax = np.abs(blocks).max(-1, keepdims=True)
    byte = np.maximum(np.where(amax > 0, np.frexp(amax)[1] - 1 + 127, 0) - down, 1)
    scale = np.exp2(byte - 127.0)
    codes = (blocks / scale).astype(np.float32).astype(dtype).astype(np.float64)
    return np.moveaxis((codes * scale).reshape(v.shape), -1, axis)


WIDE = False


def mx_kscale(k):
    if not WIDE:
        return np.ones(k)
    levels = np.array([10, -10, 5, -5, 0])
    if k % 512:
        return np.exp2(np.random.permutation(np.resize(levels, k // 32))).repeat(32)
    a = np.empty((k // 512, 16))
    for p in range(k // 512):
        a[p, :8] = np.random.permutation(np.resize(levels, 8))
        for g in range(8):
            far = levels[np.abs(levels - a[p, g]) >= 10]
            a[p, g + 8] = far[np.random.randint(len(far))]
    return np.exp2(a.ravel()).repeat(32)


def f64(x):
    return np.asarray(x).astype(np.float64)


def striped(idx):
    return np.tile(np.asarray(idx).reshape(-1, 16).T, (8, 1)).astype(np.uint16)


def unstriped(offs):
    return offs[:16].T.reshape(-1).astype(np.int64)


def striped8(idx):
    return np.asarray(idx).reshape(8, -1, 16).transpose(0, 2, 1).reshape(128, -1).astype(np.uint16)


def unstriped8(offs):
    return offs.reshape(8, 16, -1).transpose(0, 2, 1).reshape(8, -1).astype(np.int64)


def pick8(x, idx, run):
    r = np.arange(len(x))
    return x[r[:, None], idx[r % (8 * run) // run]]


E2M1 = np.array([0.0, 0.5, 1.0, 1.5, 2.0, 3.0, 4.0, 6.0, -0.0, -0.5, -1.0, -1.5, -2.0, -3.0, -4.0, -6.0])


def pack_weight(w, fmt):
    k, n = w.shape
    w = f64(np.asarray(w, np.float32).astype(ml_dtypes.bfloat16)).reshape(k // 32, 32, n)
    amax = np.abs(w).max(1)
    if fmt == "e4m3":
        byte = np.frexp(amax)[1] - 1 + 127 - 7
    else:
        mant, ex = np.frexp(amax / 6.0)
        byte = np.where(mant > 0.5, ex, ex - 1) + 127
    byte = np.clip(np.where(amax > 0, byte, 1), 1, 254)
    scaled = (w * np.exp2(127.0 - byte)[:, None, :]).reshape(k, n).astype(np.float32)
    by_word = np.ascontiguousarray(scaled.reshape(k // 512, 128, 4, n).transpose(0, 1, 3, 2))
    if fmt == "e4m3":
        words = by_word.astype(ml_dtypes.float8_e4m3fn).view(np.uint8)
    else:
        c = by_word.astype(ml_dtypes.float4_e2m1fn).view(np.uint8) & 0xF
        words = (c[..., 0::2] | (c[..., 1::2] << 4)).reshape(k // 512, 128, 2 * n)
    return np.ascontiguousarray(words), np.ascontiguousarray(byte.astype(np.uint8).reshape(k // 512, 16, n))


def unpack_weight(words, scales, fmt):
    g, _, n = scales.shape
    words = np.ascontiguousarray(words).reshape(g, 128, n, -1)
    if fmt == "e4m3":
        vals = words.view(ml_dtypes.float8_e4m3fn).astype(np.float64)
    else:
        nib = np.empty((g, 128, n, 4), np.uint8)
        nib[..., 0::2] = words & 0xF
        nib[..., 1::2] = words >> 4
        vals = E2M1[nib]
    vals = vals * np.repeat(np.exp2(scales.astype(np.float64) - 127.0), 8, axis=1)[..., None]
    return vals.transpose(0, 1, 3, 2).reshape(g * 512, n)


def sigmoid(v):
    return 1.0 / (1.0 + np.exp(-v))


def sgn(shape):
    return np.random.uniform(0.5, 2.0, shape) * np.where(np.random.standard_normal(shape) < 0, -1.0, 1.0)


K, J, R, T, Z, M, C, O, N = 512, 512, 512, 2048, 512, 1024, 1024, 512, 256


def setup_inputs():
    n = np.random.standard_normal
    idx = np.random.permutation(T)[:J]
    idx2 = np.random.permutation(M)[:J]
    idx3 = np.stack([np.random.permutation(C)[:J] for _ in range(8)])
    idx4 = np.stack([np.random.permutation(C)[:J] for _ in range(8)])
    idx5 = np.stack([np.random.permutation(C)[:O] for _ in range(8)])
    idx6 = np.stack([np.random.permutation(C)[:O] for _ in range(8)])
    fk = mx_kscale(K)
    fr = mx_kscale(R)
    fz = mx_kscale(Z)
    xtp = pack_weight(n((K, T)) * fk[:, None], "e2m1")
    wp = pack_weight(n((K, R)) * 1 / np.sqrt(K) / fk[:, None] * fr, "e4m3")
    xop = pack_weight(n((Z, M)) / fz[:, None], "e4m3")
    w2p = pack_weight(n((Z, R)) * 1 / np.sqrt(Z) * fz[:, None], "e2m1")
    wbp = pack_weight(n((R, N)) * 1 / np.sqrt(R) / fr[:, None], "e2m1")
    return {
        "xt_words": xtp[0],
        "xt_scales": xtp[1],
        "w_words": wp[0],
        "w_scales": wp[1],
        "xo_words": xop[0],
        "xo_scales": xop[1],
        "w2_words": w2p[0],
        "w2_scales": w2p[1],
        "sl": (sgn((R, 1))).astype(np.float32),
        "gf": (np.random.uniform(-1.0, 1.0, (R, 1))).astype(np.float32),
        "sa": (np.random.uniform(0.5, 1.6, (R, 1))).astype(np.float32),
        "wb_words": wbp[0],
        "wb_scales": wbp[1],
        "offs": striped(idx),
        "offs2": striped(idx2),
        "offs3": striped8(idx3),
        "offs4": striped8(idx4),
        "offs5": striped8(idx5),
        "offs6": striped8(idx6),
    }


def reference(xt_words, xt_scales, w_words, w_scales, xo_words, xo_scales, w2_words, w2_scales, sl, gf, sa, wb_words, wb_scales, offs, offs2, offs3, offs4, offs5, offs6):
    idx = unstriped(offs)
    idx2 = unstriped(offs2)
    idx3 = unstriped8(offs3)
    idx4 = unstriped8(offs4)
    idx5 = unstriped8(offs5)
    idx6 = unstriped8(offs6)
    xtu = unpack_weight(xt_words, xt_scales, "e2m1")
    wu = unpack_weight(w_words, w_scales, "e4m3")
    xou = unpack_weight(xo_words, xo_scales, "e4m3")
    w2u = unpack_weight(w2_words, w2_scales, "e2m1")
    wbu = unpack_weight(wb_words, wb_scales, "e2m1")
    xtidxg = xtu[:, idx]
    a = wu.T @ xtidxg
    xoidx2g = xou[:, idx2]
    b = w2u.T @ xoidx2g
    pw = np.zeros((R, C))
    pw[np.arange(R)[:, None], idx3[np.arange(R) % 512 // 64]] = a
    pv = np.zeros((R, C))
    pv[np.arange(R)[:, None], idx4[np.arange(R) % 512 // 64]] = b
    hid = pick8(pw, idx5, 64) * f64(sa) * sigmoid(pick8(pv, idx6, 64) * f64(sl) + f64(gf))
    hidq = mxq(hid, 0, "e4m3")
    y = wbu.T @ hidq
    return y

@@ -1,0 +1,231 @@
+from contextlib import ExitStack
+
+import concourse.mybir as mybir
+
+F32 = mybir.dt.float32
+BF16 = mybir.dt.bfloat16
+I32 = mybir.dt.int32
+U32 = mybir.dt.uint32
+U16 = mybir.dt.uint16
+U8 = mybir.dt.uint8
+FP8X4 = mybir.dt.float8_e4m3fn_x4
+FP4X4 = mybir.dt.float4_e2m1fn_x4
+COPY = mybir.ActivationFunctionType.Copy
+SIGMOID = mybir.ActivationFunctionType.Sigmoid
+MULT = mybir.AluOpType.mult
+
+P = 128
+PACK = 4
+K, J, R, T, Z, M, C, O, N = 512, 512, 512, 2048, 512, 1024, 1024, 512, 256
+HALF = O // 2
+LAST = PACK - 1
+HEAD_PIECES = ((0, 128), (128, 256), (256, J))
+FLOPS = 2 * K * R * J + 2 * Z * R * J + 2 * R * N * O
+
+
+def cols16(lo, hi):
+    return slice(lo // 16, hi // 16)
+
+
+def tile_picked_tokens_gate_two_sigmoidboard_one_plain_kernel(
+    tc, xt_words, xt_scales, w_words, w_scales, xo_words, xo_scales, w2_words, w2_scales,
+    sl, gf, sa, wb_words, wb_scales, offs, offs2, offs3, offs4, offs5, offs6, out,
+):
+    nc = tc.nc
+    with ExitStack() as ctx:
+        keep = ctx.enter_context(tc.tile_pool(name="keep", bufs=1))
+        psum = ctx.enter_context(tc.psum_pool(name="psum", bufs=8))
+
+        def load_list(src, name):
+            tile = keep.tile([P, J // 16], U16, name=name)
+            nc.sync.dma_start(tile[:], src)
+            return tile
+
+        def load_scales(plane, src):
+            rows = src[0].bitcast(I32)
+            for q in range(4):
+                nc.sync.dma_start(plane[32 * q : 32 * q + 4, :].bitcast(I32), rows[4 * q : 4 * q + 4, :])
+
+        def load_rows(src, name):
+            tile = keep.tile([P, PACK], F32, name=name)
+            nc.sync.dma_start(tile[:], src.rearrange("(p t) one -> p (t one)", t=PACK))
+            return tile
+
+        def board(name, tag, engine):
+            tile = keep.tile([P, C], F32, name=name, tag=tag, align_bytes=64)
+            engine.memset(tile[:], 0.0)
+            return tile
+
+        def stage_scales(src, width, name):
+            stage = keep.tile([4, 4, width // 4], I32, name=name)
+            nc.scalar.dma_start(stage[:], src[0].bitcast(I32).rearrange("(q r) c -> r q c", r=4))
+            return stage
+
+        def zero_plane(width, name, tag):
+            plane = keep.tile([P, width], U8, name=name, tag=tag, align_bytes=64)
+            nc.vector.memset(plane[:].bitcast(I32), 0)
+            return plane
+
+        xo_w = keep.tile([P, M], U32, name="xo_w", tag="slot_a", align_bytes=64)
+        nc.sync.dma_start(xo_w[:].bitcast(I32), xo_words[0].rearrange("p n t -> p (n t)").bitcast(I32))
+        w2_stage = stage_scales(w2_scales, R, "w2_stage")
+        xo_stage = stage_scales(xo_scales, M, "xo_stage")
+        list2 = load_list(offs2, "list2")
+        w2_w = keep.tile([P, R], U16, name="w2_w", align_bytes=64)
+        nc.sync.dma_start(w2_w[:].bitcast(I32), w2_words[0].bitcast(I32))
+        xo_s = zero_plane(M, "xo_s", "table_scales")
+        w2_s = zero_plane(R, "w2_s", "weight_scales")
+        list4 = load_list(offs4, "list4")
+        pv = [board("pv0", "pv0", nc.vector), board("pv1", "pv1", nc.gpsimd)]
+        list6 = load_list(offs6, "list6")
+        sl_t = load_rows(sl, "sl_t")
+        gf_t = load_rows(gf, "gf_t")
+        list1 = load_list(offs, "list1")
+        xt_w = keep.tile([P, T], U16, name="xt_w", tag="slot_b", align_bytes=64)
+        nc.sync.dma_start(xt_w[:].bitcast(I32), xt_words[0].bitcast(I32))
+        w_w = keep.tile([P, R], U32, name="w_w", align_bytes=64)
+        nc.sync.dma_start(w_w[:].bitcast(I32), w_words[0].rearrange("p n t -> p (n t)").bitcast(I32))
+        list3 = load_list(offs3, "list3")
+        list5 = load_list(offs5, "list5")
+        sa_t = load_rows(sa, "sa_t")
+        wb_w = keep.tile([P, N], U16, name="wb_w", align_bytes=64)
+        nc.sync.dma_start(wb_w[:].bitcast(I32), wb_words[0].bitcast(I32))
+        wb_s = zero_plane(N, "wb_s", "wb_s")
+        load_scales(wb_s, wb_scales)
+
+        for q in range(4):
+            nc.vector.tensor_copy(w2_s[32 * q : 32 * q + 4, :].bitcast(I32), w2_stage[:, q, :])
+            nc.vector.tensor_copy(xo_s[32 * q : 32 * q + 4, :].bitcast(I32), xo_stage[:, q, :])
+        w2_d = keep.tile([P, PACK, P], U16, name="w2_d", tag="lhs_words", align_bytes=64)
+        w2_words_by_t = w2_w[:].rearrange("p (m t) -> p t m", t=PACK)
+        nc.scalar.copy(w2_d[:, 0, :], w2_words_by_t[:, 0, :])
+        w2_ds = keep.tile([P, PACK, P], U8, name="w2_ds", tag="lhs_scales", align_bytes=64)
+        w2_by_t = w2_s[:].rearrange("p (m t) -> p t m", t=PACK)
+        nc.vector.tensor_copy(w2_ds[:, 0, :], w2_by_t[:, 0, :])
+        xog_s = keep.tile([P, J], U8, name="xog_s", tag="rhs_scales", align_bytes=64)
+        xog_w = keep.tile([P, J], U32, name="xog_w", tag="rhs_words", align_bytes=64)
+        b_sb = [keep.tile([P, J], F32, name=f"b_sb{t}") for t in range(PACK)]
+
+        def product_b(t, lo, hi):
+            acc = psum.tile([P, J], F32, name="acc_b", tag="bank")
+            nc.tensor.matmul_mx(
+                out=acc[:, lo:hi], lhsT=w2_d[:, t, :].bitcast(FP4X4), lhsT_scale=w2_ds[:, t, :],
+                rhs=xog_w[:, lo:hi].bitcast(FP8X4), rhs_scale=xog_s[:, lo:hi], start=True, stop=True,
+            )
+            return acc[:, lo:hi]
+
+        for lo, hi in HEAD_PIECES:
+            nc.vector.tensor_copy(xog_s[:, lo:hi], xo_s[:].indirect(list2[:, cols16(lo, hi)]))
+            nc.vector.tensor_copy(xog_w[:, lo:hi], xo_w[:].indirect(list2[:, cols16(lo, hi)]))
+            acc = product_b(0, lo, hi)
+            if hi < J:
+                nc.scalar.copy(b_sb[0][:, lo:hi], acc)
+            else:
+                nc.vector.tensor_copy(b_sb[0][:, lo:hi], acc)
+            nc.scalar.activation(pv[0][:].indirect(list4[:, cols16(lo, hi)]), b_sb[0][:, lo:hi], COPY)
+
+        nc.scalar.copy(w2_d[:, 1:, :], w2_words_by_t[:, 1:, :])
+        nc.vector.tensor_copy(w2_ds[:, 1:, :], w2_by_t[:, 1:, :])
+        for t in range(1, PACK):
+            nc.vector.tensor_copy(b_sb[t][:], product_b(t, 0, J))
+
+        xt_s = zero_plane(T, "xt_s", "table_scales")
+        load_scales(xt_s, xt_scales)
+        w_s = w2_s
+        load_scales(w_s, w_scales)
+        xtg_s = keep.tile([P, J], U8, name="xtg_s", tag="rhs_scales", align_bytes=64)
+        xtg_w = keep.tile([P, J], U16, name="xtg_w", tag="rhs_words", align_bytes=64)
+        nc.vector.tensor_copy(xtg_w[:], xt_w[:].indirect(list1[:]))
+        nc.vector.tensor_copy(xtg_s[:], xt_s[:].indirect(list1[:]))
+        w_d = keep.tile([P, PACK, P], U32, name="w_d", tag="lhs_words", align_bytes=64)
+        nc.vector.tensor_copy(w_d[:].bitcast(I32), w_w[:].bitcast(I32).rearrange("p (m t) -> p t m", t=PACK))
+        w_ds = keep.tile([P, PACK, P], U8, name="w_ds", tag="lhs_scales", align_bytes=64)
+        nc.vector.tensor_copy(w_ds[:], w_s[:].rearrange("p (m t) -> p t m", t=PACK))
+        a_sb = [[keep.tile([P, HALF], F32, name=f"a_sb{t}{h}") for h in range(2)] if t == LAST
+                else keep.tile([P, J], F32, name=f"a_sb{t}") for t in range(PACK)]
+        for t in range(PACK):
+            acc = psum.tile([P, J], F32, name="acc_a", tag="bank")
+            nc.tensor.matmul_mx(
+                out=acc[:], lhsT=w_d[:, t, :].bitcast(FP8X4), lhsT_scale=w_ds[:, t, :],
+                rhs=xtg_w[:].bitcast(FP4X4), rhs_scale=xtg_s[:], start=True, stop=True,
+            )
+            if t == LAST:
+                for h in range(2):
+                    nc.vector.tensor_copy(a_sb[t][h][:], acc[:, h * HALF : (h + 1) * HALF])
+            else:
+                nc.vector.tensor_copy(a_sb[t][:], acc[:])
+        pw = [board("pw0", "slot_b", nc.vector), board("pw1", "slot_a", nc.vector)]
+
+        gate = [keep.tile([P, O], F32, name=f"gate{t}") for t in range(LAST)]
+        value = [keep.tile([P, O], F32, name=f"value{t}") for t in range(PACK)]
+        hid = [keep.tile([P, HALF, PACK], BF16, name=f"hid{h}", align_bytes=64) for h in range(2)]
+
+        def put_gate(t):
+            nc.scalar.activation(pv[t % 2][:].indirect(list4[:]), b_sb[t][:], COPY)
+
+        def put_value(t):
+            nc.scalar.activation(pw[t % 2][:].indirect(list3[:]), a_sb[t][:], COPY)
+
+        def get_gate(t, lo, hi, dst):
+            nc.scalar.activation(
+                dst, pv[t % 2][:].indirect(list6[:, cols16(lo, hi)]), SIGMOID,
+                scale=sl_t[:, t : t + 1], bias=gf_t[:, t : t + 1],
+            )
+
+        def get_value(t, lo, hi):
+            nc.scalar.activation(
+                value[t][:, lo:hi], pw[t % 2][:].indirect(list5[:, cols16(lo, hi)]), COPY,
+                scale=sa_t[:, t : t + 1],
+            )
+
+        def multiply(t, h, gates):
+            cols = slice(h * HALF, (h + 1) * HALF)
+            nc.vector.tensor_tensor(hid[h][:, :, t], value[t][:, cols], gates, MULT)
+
+        def finish(h):
+            codes = keep.tile([P, HALF], U32, name=f"codes{h}", align_bytes=64)
+            scales = keep.tile([P, HALF], U8, name=f"scales{h}", align_bytes=64)
+            nc.vector.quantize_mx(
+                out=codes[:].bitcast(FP8X4), scales=scales[:], in_=hid[h][:].rearrange("p o t -> p (o t)")
+            )
+            res = keep.tile([P, 2, HALF], F32, name=f"res{h}")
+            for n in range(2):
+                acc = psum.tile([P, J], F32, name=f"acc_o{h}{n}", tag="bank")
+                nc.tensor.matmul_mx(
+                    out=acc[:, :HALF], lhsT=wb_w[:, n * P : (n + 1) * P].bitcast(FP4X4),
+                    lhsT_scale=wb_s[:, n * P : (n + 1) * P],
+                    rhs=codes[:].bitcast(FP8X4), rhs_scale=scales[:], start=True, stop=True,
+                )
+                if n == 0 or h == 0:
+                    nc.vector.tensor_copy(res[:, n, :], acc[:, :HALF])
+                else:
+                    nc.scalar.copy(res[:, n, :], acc[:, :HALF])
+            nc.sync.dma_start(out.rearrange("(n p) o -> p n o", p=P)[:, :, h * HALF : (h + 1) * HALF], res[:])
+
+        def value_and_products(t):
+            get_value(t, 0, O)
+            for h in range(2):
+                multiply(t, h, gate[t][:, h * HALF : (h + 1) * HALF])
+
+        def put_last_value(h):
+            nc.scalar.activation(
+                pw[LAST % 2][:].indirect(list3[:, cols16(h * HALF, (h + 1) * HALF)]), a_sb[LAST][h][:], COPY
+            )
+
+        for t in range(1, PACK):
+            put_gate(t)
+            get_gate(t - 1, 0, O, gate[t - 1][:])
+        put_value(0)
+        put_value(1)
+        value_and_products(0)
+        value_and_products(1)
+        put_value(2)
+        put_last_value(0)
+        value_and_products(2)
+        put_last_value(1)
+        for h in range(2):
+            last_gate = keep.tile([P, HALF], F32, name="last_gate", tag=f"a_sb{LAST}{h}")
+            get_gate(LAST, h * HALF, (h + 1) * HALF, last_gate[:])
+            get_value(LAST, h * HALF, (h + 1) * HALF)
+            multiply(LAST, h, last_gate[:])
+            finish(h)

@@ -19,6 +19,7 @@ PACK = 4
 K, J, R, T, Z, M, C, O, N = 512, 512, 512, 2048, 512, 1024, 1024, 512, 256
 HALF = O // 2
 LAST = PACK - 1
+OUT_PIECES = ((0, HALF), (HALF, HALF + 128), (HALF + 128, O))
 HEAD_PIECES = ((0, 128), (128, 256), (256, J))
 FLOPS = 2 * K * R * J + 2 * Z * R * J + 2 * R * N * O
 
@@ -58,7 +59,7 @@ def tile_picked_tokens_gate_two_sigmoidboard_one_plain_kernel(
 
         def stage_scales(src, width, name):
             stage = keep.tile([4, 4, width // 4], I32, name=name)
-            nc.scalar.dma_start(stage[:], src[0].bitcast(I32).rearrange("(q r) c -> r q c", r=4))
+            nc.sync.dma_start(stage[:], src[0].bitcast(I32).rearrange("(q r) c -> r q c", r=4))
             return stage
 
         def zero_plane(width, name, tag):
@@ -66,13 +67,13 @@ def tile_picked_tokens_gate_two_sigmoidboard_one_plain_kernel(
             nc.vector.memset(plane[:].bitcast(I32), 0)
             return plane
 
-        xo_w = keep.tile([P, M], U32, name="xo_w", tag="slot_a", align_bytes=64)
-        nc.sync.dma_start(xo_w[:].bitcast(I32), xo_words[0].rearrange("p n t -> p (n t)").bitcast(I32))
-        w2_stage = stage_scales(w2_scales, R, "w2_stage")
         xo_stage = stage_scales(xo_scales, M, "xo_stage")
-        list2 = load_list(offs2, "list2")
+        w2_stage = stage_scales(w2_scales, R, "w2_stage")
         w2_w = keep.tile([P, R], U16, name="w2_w", align_bytes=64)
         nc.sync.dma_start(w2_w[:].bitcast(I32), w2_words[0].bitcast(I32))
+        xo_w = keep.tile([P, M], U32, name="xo_w", align_bytes=64)
+        nc.sync.dma_start(xo_w[:].bitcast(I32), xo_words[0].rearrange("p n t -> p (n t)").bitcast(I32))
+        list2 = load_list(offs2, "list2")
         xo_s = zero_plane(M, "xo_s", "table_scales")
         w2_s = zero_plane(R, "w2_s", "weight_scales")
         list4 = load_list(offs4, "list4")
@@ -94,14 +95,14 @@ def tile_picked_tokens_gate_two_sigmoidboard_one_plain_kernel(
         load_scales(wb_s, wb_scales)
 
         for q in range(4):
-            nc.vector.tensor_copy(w2_s[32 * q : 32 * q + 4, :].bitcast(I32), w2_stage[:, q, :])
             nc.vector.tensor_copy(xo_s[32 * q : 32 * q + 4, :].bitcast(I32), xo_stage[:, q, :])
+            nc.vector.tensor_copy(w2_s[32 * q : 32 * q + 4, :].bitcast(I32), w2_stage[:, q, :])
         w2_d = keep.tile([P, PACK, P], U16, name="w2_d", tag="lhs_words", align_bytes=64)
         w2_words_by_t = w2_w[:].rearrange("p (m t) -> p t m", t=PACK)
         nc.scalar.copy(w2_d[:, 0, :], w2_words_by_t[:, 0, :])
-        w2_ds = keep.tile([P, PACK, P], U8, name="w2_ds", tag="lhs_scales", align_bytes=64)
+        w2_ds0 = keep.tile([P, P], U8, name="w2_ds0", tag="lhs_scales", align_bytes=64)
+        w2_ds = [w2_ds0[:]]
         w2_by_t = w2_s[:].rearrange("p (m t) -> p t m", t=PACK)
-        nc.vector.tensor_copy(w2_ds[:, 0, :], w2_by_t[:, 0, :])
         xog_s = keep.tile([P, J], U8, name="xog_s", tag="rhs_scales", align_bytes=64)
         xog_w = keep.tile([P, J], U32, name="xog_w", tag="rhs_words", align_bytes=64)
         b_sb = [keep.tile([P, J], F32, name=f"b_sb{t}") for t in range(PACK)]
@@ -109,7 +110,7 @@ def tile_picked_tokens_gate_two_sigmoidboard_one_plain_kernel(
         def product_b(t, lo, hi):
             acc = psum.tile([P, J], F32, name="acc_b", tag="bank")
             nc.tensor.matmul_mx(
-                out=acc[:, lo:hi], lhsT=w2_d[:, t, :].bitcast(FP4X4), lhsT_scale=w2_ds[:, t, :],
+                out=acc[:, lo:hi], lhsT=w2_d[:, t, :].bitcast(FP4X4), lhsT_scale=w2_ds[t],
                 rhs=xog_w[:, lo:hi].bitcast(FP8X4), rhs_scale=xog_s[:, lo:hi], start=True, stop=True,
             )
             return acc[:, lo:hi]
@@ -117,6 +118,8 @@ def tile_picked_tokens_gate_two_sigmoidboard_one_plain_kernel(
         for lo, hi in HEAD_PIECES:
             nc.vector.tensor_copy(xog_s[:, lo:hi], xo_s[:].indirect(list2[:, cols16(lo, hi)]))
             nc.vector.tensor_copy(xog_w[:, lo:hi], xo_w[:].indirect(list2[:, cols16(lo, hi)]))
+            if lo == 0:
+                nc.vector.tensor_copy(w2_ds[0], w2_by_t[:, 0, :])
             acc = product_b(0, lo, hi)
             if hi < J:
                 nc.scalar.copy(b_sb[0][:, lo:hi], acc)
@@ -125,7 +128,9 @@ def tile_picked_tokens_gate_two_sigmoidboard_one_plain_kernel(
             nc.scalar.activation(pv[0][:].indirect(list4[:, cols16(lo, hi)]), b_sb[0][:, lo:hi], COPY)
 
         nc.scalar.copy(w2_d[:, 1:, :], w2_words_by_t[:, 1:, :])
-        nc.vector.tensor_copy(w2_ds[:, 1:, :], w2_by_t[:, 1:, :])
+        w2_rest = keep.tile([P, LAST, P], U8, name="w2_rest", tag="table_scales", align_bytes=64)
+        nc.vector.tensor_copy(w2_rest[:], w2_by_t[:, 1:, :])
+        w2_ds.extend(w2_rest[:, t, :] for t in range(LAST))
         for t in range(1, PACK):
             nc.vector.tensor_copy(b_sb[t][:], product_b(t, 0, J))
 
@@ -154,11 +159,11 @@ def tile_picked_tokens_gate_two_sigmoidboard_one_plain_kernel(
                     nc.vector.tensor_copy(a_sb[t][h][:], acc[:, h * HALF : (h + 1) * HALF])
             else:
                 nc.vector.tensor_copy(a_sb[t][:], acc[:])
-        pw = [board("pw0", "slot_b", nc.vector), board("pw1", "slot_a", nc.vector)]
+        pw = [board("pw0", "slot_b", nc.vector), board("pw1", "rhs_words", nc.vector)]
 
         gate = [keep.tile([P, O], F32, name=f"gate{t}") for t in range(LAST)]
         value = [keep.tile([P, O], F32, name=f"value{t}") for t in range(PACK)]
-        hid = [keep.tile([P, HALF, PACK], BF16, name=f"hid{h}", align_bytes=64) for h in range(2)]
+        hid = [keep.tile([P, hi - lo, PACK], BF16, name=f"hid{lo}", align_bytes=64) for lo, hi in OUT_PIECES]
 
         def put_gate(t):
             nc.scalar.activation(pv[t % 2][:].indirect(list4[:]), b_sb[t][:], COPY)
@@ -178,34 +183,41 @@ def tile_picked_tokens_gate_two_sigmoidboard_one_plain_kernel(
                 scale=sa_t[:, t : t + 1],
             )
 
-        def multiply(t, h, gates):
-            cols = slice(h * HALF, (h + 1) * HALF)
-            nc.vector.tensor_tensor(hid[h][:, :, t], value[t][:, cols], gates, MULT)
+        def multiply(t, i, gates):
+            lo, hi = OUT_PIECES[i]
+            nc.vector.tensor_tensor(hid[i][:, :, t], value[t][:, lo:hi], gates, MULT)
 
-        def finish(h):
-            codes = keep.tile([P, HALF], U32, name=f"codes{h}", align_bytes=64)
-            scales = keep.tile([P, HALF], U8, name=f"scales{h}", align_bytes=64)
+        def finish(i):
+            lo, hi = OUT_PIECES[i]
+            width = hi - lo
+            codes = keep.tile([P, width], U32, name=f"codes{i}", align_bytes=64)
+            scales = keep.tile([P, width], U8, name=f"scales{i}", align_bytes=64)
             nc.vector.quantize_mx(
-                out=codes[:].bitcast(FP8X4), scales=scales[:], in_=hid[h][:].rearrange("p o t -> p (o t)")
+                out=codes[:].bitcast(FP8X4), scales=scales[:], in_=hid[i][:].rearrange("p o t -> p (o t)")
             )
-            res = keep.tile([P, 2, HALF], F32, name=f"res{h}")
+            res = keep.tile([P, 2, width], F32, name=f"res{i}")
+            split = hi == O
+            acc = None
             for n in range(2):
-                acc = psum.tile([P, J], F32, name=f"acc_o{h}{n}", tag="bank")
+                if n == 0 or split:
+                    acc = psum.tile([P, 2, HALF], F32, name="acc_o", tag="bank")
                 nc.tensor.matmul_mx(
-                    out=acc[:, :HALF], lhsT=wb_w[:, n * P : (n + 1) * P].bitcast(FP4X4),
+                    out=acc[:, n, :width], lhsT=wb_w[:, n * P : (n + 1) * P].bitcast(FP4X4),
                     lhsT_scale=wb_s[:, n * P : (n + 1) * P],
                     rhs=codes[:].bitcast(FP8X4), rhs_scale=scales[:], start=True, stop=True,
                 )
-                if n == 0 or h == 0:
-                    nc.vector.tensor_copy(res[:, n, :], acc[:, :HALF])
-                else:
-                    nc.scalar.copy(res[:, n, :], acc[:, :HALF])
-            nc.sync.dma_start(out.rearrange("(n p) o -> p n o", p=P)[:, :, h * HALF : (h + 1) * HALF], res[:])
+                if split and n == 0:
+                    nc.vector.tensor_copy(res[:, n, :], acc[:, n, :width])
+                elif split:
+                    nc.scalar.copy(res[:, n, :], acc[:, n, :width])
+            if not split:
+                nc.scalar.copy(res[:], acc[:, :, :width])
+            nc.sync.dma_start(out.rearrange("(n p) o -> p n o", p=P)[:, :, lo:hi], res[:])
 
         def value_and_products(t):
             get_value(t, 0, O)
-            for h in range(2):
-                multiply(t, h, gate[t][:, h * HALF : (h + 1) * HALF])
+            for i, (lo, hi) in enumerate(OUT_PIECES):
+                multiply(t, i, gate[t][:, lo:hi])
 
         def put_last_value(h):
             nc.scalar.activation(
@@ -227,5 +239,8 @@ def tile_picked_tokens_gate_two_sigmoidboard_one_plain_kernel(
             last_gate = keep.tile([P, HALF], F32, name="last_gate", tag=f"a_sb{LAST}{h}")
             get_gate(LAST, h * HALF, (h + 1) * HALF, last_gate[:])
             get_value(LAST, h * HALF, (h + 1) * HALF)
-            multiply(LAST, h, last_gate[:])
-            finish(h)
+            for i, (lo, hi) in enumerate(OUT_PIECES):
+                if lo // HALF == h:
+                    multiply(LAST, i, last_gate[:, lo - h * HALF : hi - h * HALF])
+        for i in range(len(OUT_PIECES)):
+            finish(i)

@@ -19,7 +19,7 @@ PACK = 4
 K, J, R, T, Z, M, C, O, N = 512, 512, 512, 2048, 512, 1024, 1024, 512, 256
 HALF = O // 2
 LAST = PACK - 1
-OUT_PIECES = ((0, HALF), (HALF, HALF + 128), (HALF + 128, O))
+OUT_PIECES = tuple((lo, lo + 128) for lo in range(0, O, 128))
 HEAD_PIECES = ((0, 128), (128, 256), (256, J))
 FLOPS = 2 * K * R * J + 2 * Z * R * J + 2 * R * N * O
 
@@ -67,6 +67,11 @@ def tile_picked_tokens_gate_two_sigmoidboard_one_plain_kernel(
             nc.vector.memset(plane[:].bitcast(I32), 0)
             return plane
 
+        warm_in = keep.tile([P, 1], F32, name="warm_in")
+        warm_out = keep.tile([P, 1], F32, name="warm_out")
+        nc.vector.memset(warm_in[:], 0.0)
+        nc.scalar.activation(warm_out[:], warm_in[:], SIGMOID)
+
         xo_stage = stage_scales(xo_scales, M, "xo_stage")
         w2_stage = stage_scales(w2_scales, R, "w2_stage")
         w2_w = keep.tile([P, R], U16, name="w2_w", align_bytes=64)
@@ -97,9 +102,12 @@ def tile_picked_tokens_gate_two_sigmoidboard_one_plain_kernel(
         for q in range(4):
             nc.vector.tensor_copy(xo_s[32 * q : 32 * q + 4, :].bitcast(I32), xo_stage[:, q, :])
             nc.vector.tensor_copy(w2_s[32 * q : 32 * q + 4, :].bitcast(I32), w2_stage[:, q, :])
-        w2_d = keep.tile([P, PACK, P], U16, name="w2_d", tag="lhs_words", align_bytes=64)
+        w2_d0 = keep.tile([P, P], U16, name="w2_d0", align_bytes=64)
+        w2_d123 = keep.tile([P, LAST, P], U16, name="w2_d123", tag="lhs_words", align_bytes=64)
+        w2_d = [w2_d0[:]] + [w2_d123[:, t, :] for t in range(LAST)]
         w2_words_by_t = w2_w[:].rearrange("p (m t) -> p t m", t=PACK)
-        nc.scalar.copy(w2_d[:, 0, :], w2_words_by_t[:, 0, :])
+        nc.scalar.copy(w2_d0[:], w2_words_by_t[:, 0, :])
+        nc.scalar.copy(w2_d123[:], w2_words_by_t[:, 1:, :])
         w2_ds0 = keep.tile([P, P], U8, name="w2_ds0", tag="lhs_scales", align_bytes=64)
         w2_ds = [w2_ds0[:]]
         w2_by_t = w2_s[:].rearrange("p (m t) -> p t m", t=PACK)
@@ -110,7 +118,7 @@ def tile_picked_tokens_gate_two_sigmoidboard_one_plain_kernel(
         def product_b(t, lo, hi):
             acc = psum.tile([P, J], F32, name="acc_b", tag="bank")
             nc.tensor.matmul_mx(
-                out=acc[:, lo:hi], lhsT=w2_d[:, t, :].bitcast(FP4X4), lhsT_scale=w2_ds[t],
+                out=acc[:, lo:hi], lhsT=w2_d[t].bitcast(FP4X4), lhsT_scale=w2_ds[t],
                 rhs=xog_w[:, lo:hi].bitcast(FP8X4), rhs_scale=xog_s[:, lo:hi], start=True, stop=True,
             )
             return acc[:, lo:hi]
@@ -127,7 +135,6 @@ def tile_picked_tokens_gate_two_sigmoidboard_one_plain_kernel(
                 nc.vector.tensor_copy(b_sb[0][:, lo:hi], acc)
             nc.scalar.activation(pv[0][:].indirect(list4[:, cols16(lo, hi)]), b_sb[0][:, lo:hi], COPY)
 
-        nc.scalar.copy(w2_d[:, 1:, :], w2_words_by_t[:, 1:, :])
         w2_rest = keep.tile([P, LAST, P], U8, name="w2_rest", tag="table_scales", align_bytes=64)
         nc.vector.tensor_copy(w2_rest[:], w2_by_t[:, 1:, :])
         w2_ds.extend(w2_rest[:, t, :] for t in range(LAST))
@@ -142,6 +149,7 @@ def tile_picked_tokens_gate_two_sigmoidboard_one_plain_kernel(
         xtg_w = keep.tile([P, J], U16, name="xtg_w", tag="rhs_words", align_bytes=64)
         nc.vector.tensor_copy(xtg_w[:], xt_w[:].indirect(list1[:]))
         nc.vector.tensor_copy(xtg_s[:], xt_s[:].indirect(list1[:]))
+        pw = [board("pw0", "slot_b", nc.vector), board("pw1", "table_scales", nc.vector)]
         w_d = keep.tile([P, PACK, P], U32, name="w_d", tag="lhs_words", align_bytes=64)
         nc.vector.tensor_copy(w_d[:].bitcast(I32), w_w[:].bitcast(I32).rearrange("p (m t) -> p t m", t=PACK))
         w_ds = keep.tile([P, PACK, P], U8, name="w_ds", tag="lhs_scales", align_bytes=64)
@@ -159,7 +167,6 @@ def tile_picked_tokens_gate_two_sigmoidboard_one_plain_kernel(
                     nc.vector.tensor_copy(a_sb[t][h][:], acc[:, h * HALF : (h + 1) * HALF])
             else:
                 nc.vector.tensor_copy(a_sb[t][:], acc[:])
-        pw = [board("pw0", "slot_b", nc.vector), board("pw1", "rhs_words", nc.vector)]
 
         gate = [keep.tile([P, O], F32, name=f"gate{t}") for t in range(LAST)]
         value = [keep.tile([P, O], F32, name=f"value{t}") for t in range(PACK)]
@@ -242,5 +249,6 @@ def tile_picked_tokens_gate_two_sigmoidboard_one_plain_kernel(
             for i, (lo, hi) in enumerate(OUT_PIECES):
                 if lo // HALF == h:
                     multiply(LAST, i, last_gate[:, lo - h * HALF : hi - h * HALF])
-        for i in range(len(OUT_PIECES)):
-            finish(i)
+            for i, (lo, hi) in enumerate(OUT_PIECES):
+                if lo // HALF == h:
+                    finish(i)

@@ -58,9 +58,11 @@ def tile_picked_tokens_gate_two_sigmoidboard_one_plain_kernel(
             return tile
 
         def stage_scales(src, width, name):
-            stage = keep.tile([4, 4, width // 4], I32, name=name)
-            nc.sync.dma_start(stage[:], src[0].bitcast(I32).rearrange("(q r) c -> r q c", r=4))
-            return stage
+            stage = keep.tile([P, 2, width // 4], I32, name=name)
+            rows = src[0].bitcast(I32).rearrange("(q r) c -> r q c", r=4)
+            nc.sync.dma_start(stage[0:4], rows[:, 0:2, :])
+            nc.scalar.dma_start(stage[64:68], rows[:, 2:4, :])
+            return [stage[64 * (q // 2) : 64 * (q // 2) + 4, q % 2, :] for q in range(4)]
 
         def zero_plane(width, name, tag):
             plane = keep.tile([P, width], U8, name=name, tag=tag, align_bytes=64)
@@ -100,8 +102,8 @@ def tile_picked_tokens_gate_two_sigmoidboard_one_plain_kernel(
         load_scales(wb_s, wb_scales)
 
         for q in range(4):
-            nc.vector.tensor_copy(xo_s[32 * q : 32 * q + 4, :].bitcast(I32), xo_stage[:, q, :])
-            nc.vector.tensor_copy(w2_s[32 * q : 32 * q + 4, :].bitcast(I32), w2_stage[:, q, :])
+            nc.vector.tensor_copy(xo_s[32 * q : 32 * q + 4, :].bitcast(I32), xo_stage[q])
+            nc.vector.tensor_copy(w2_s[32 * q : 32 * q + 4, :].bitcast(I32), w2_stage[q])
         w2_d0 = keep.tile([P, P], U16, name="w2_d0", align_bytes=64)
         w2_d123 = keep.tile([P, LAST, P], U16, name="w2_d123", tag="lhs_words", align_bytes=64)
         w2_d = [w2_d0[:]] + [w2_d123[:, t, :] for t in range(LAST)]

from contextlib import ExitStack

import concourse.mybir as mybir

F32 = mybir.dt.float32
BF16 = mybir.dt.bfloat16
I32 = mybir.dt.int32
U32 = mybir.dt.uint32
U16 = mybir.dt.uint16
U8 = mybir.dt.uint8
FP8X4 = mybir.dt.float8_e4m3fn_x4
FP4X4 = mybir.dt.float4_e2m1fn_x4
COPY = mybir.ActivationFunctionType.Copy
SIGMOID = mybir.ActivationFunctionType.Sigmoid
MULT = mybir.AluOpType.mult

P = 128
PACK = 4
K, J, R, T, Z, M, C, O, N = 512, 512, 512, 2048, 512, 1024, 1024, 512, 256
HALF = O // 2
LAST = PACK - 1
OUT_PIECES = tuple((lo, lo + 128) for lo in range(0, O, 128))
HEAD_PIECES = ((0, 128), (128, 256), (256, J))
FLOPS = 2 * K * R * J + 2 * Z * R * J + 2 * R * N * O


def cols16(lo, hi):
    return slice(lo // 16, hi // 16)


def tile_picked_tokens_gate_two_sigmoidboard_one_plain_kernel(
    tc, xt_words, xt_scales, w_words, w_scales, xo_words, xo_scales, w2_words, w2_scales,
    sl, gf, sa, wb_words, wb_scales, offs, offs2, offs3, offs4, offs5, offs6, out,
):
    nc = tc.nc
    with ExitStack() as ctx:
        keep = ctx.enter_context(tc.tile_pool(name="keep", bufs=1))
        psum = ctx.enter_context(tc.psum_pool(name="psum", bufs=8))

        def load_list(src, name):
            tile = keep.tile([P, J // 16], U16, name=name)
            nc.sync.dma_start(tile[:], src)
            return tile

        def load_scales(plane, src):
            rows = src[0].bitcast(I32)
            for q in range(4):
                nc.sync.dma_start(plane[32 * q : 32 * q + 4, :].bitcast(I32), rows[4 * q : 4 * q + 4, :])

        def load_rows(src, name):
            tile = keep.tile([P, PACK], F32, name=name)
            nc.sync.dma_start(tile[:], src.rearrange("(p t) one -> p (t one)", t=PACK))
            return tile

        def board(name, tag, engine):
            tile = keep.tile([P, C], F32, name=name, tag=tag, align_bytes=64)
            engine.memset(tile[:], 0.0)
            return tile

        def stage_scales(src, width, name):
            stage = keep.tile([P, 2, width // 4], I32, name=name)
            rows = src[0].bitcast(I32).rearrange("(q r) c -> r q c", r=4)
            nc.sync.dma_start(stage[0:4], rows[:, 0:2, :])
            nc.scalar.dma_start(stage[64:68], rows[:, 2:4, :])
            return [stage[64 * (q // 2) : 64 * (q // 2) + 4, q % 2, :] for q in range(4)]

        def zero_plane(width, name, tag):
            plane = keep.tile([P, width], U8, name=name, tag=tag, align_bytes=64)
            nc.vector.memset(plane[:].bitcast(I32), 0)
            return plane

        warm_in = keep.tile([P, 1], F32, name="warm_in")
        warm_out = keep.tile([P, 1], F32, name="warm_out")
        nc.vector.memset(warm_in[:], 0.0)
        nc.scalar.activation(warm_out[:], warm_in[:], SIGMOID)

        xo_stage = stage_scales(xo_scales, M, "xo_stage")
        w2_stage = stage_scales(w2_scales, R, "w2_stage")
        w2_w = keep.tile([P, R], U16, name="w2_w", align_bytes=64)
        nc.sync.dma_start(w2_w[:].bitcast(I32), w2_words[0].bitcast(I32))
        xo_w = keep.tile([P, M], U32, name="xo_w", align_bytes=64)
        nc.sync.dma_start(xo_w[:].bitcast(I32), xo_words[0].rearrange("p n t -> p (n t)").bitcast(I32))
        list2 = load_list(offs2, "list2")
        xo_s = zero_plane(M, "xo_s", "table_scales")
        w2_s = zero_plane(R, "w2_s", "weight_scales")
        list4 = load_list(offs4, "list4")
        pv = [board("pv0", "pv0", nc.vector), board("pv1", "pv1", nc.gpsimd)]
        list6 = load_list(offs6, "list6")
        sl_t = load_rows(sl, "sl_t")
        gf_t = load_rows(gf, "gf_t")
        list1 = load_list(offs, "list1")
        xt_w = keep.tile([P, T], U16, name="xt_w", tag="slot_b", align_bytes=64)
        nc.sync.dma_start(xt_w[:].bitcast(I32), xt_words[0].bitcast(I32))
        w_w = keep.tile([P, R], U32, name="w_w", align_bytes=64)
        nc.sync.dma_start(w_w[:].bitcast(I32), w_words[0].rearrange("p n t -> p (n t)").bitcast(I32))
        list3 = load_list(offs3, "list3")
        list5 = load_list(offs5, "list5")
        sa_t = load_rows(sa, "sa_t")
        wb_w = keep.tile([P, N], U16, name="wb_w", align_bytes=64)
        nc.sync.dma_start(wb_w[:].bitcast(I32), wb_words[0].bitcast(I32))
        wb_s = zero_plane(N, "wb_s", "wb_s")
        load_scales(wb_s, wb_scales)

        for q in range(4):
            nc.vector.tensor_copy(xo_s[32 * q : 32 * q + 4, :].bitcast(I32), xo_stage[q])
            nc.vector.tensor_copy(w2_s[32 * q : 32 * q + 4, :].bitcast(I32), w2_stage[q])
        w2_d0 = keep.tile([P, P], U16, name="w2_d0", align_bytes=64)
        w2_d123 = keep.tile([P, LAST, P], U16, name="w2_d123", tag="lhs_words", align_bytes=64)
        w2_d = [w2_d0[:]] + [w2_d123[:, t, :] for t in range(LAST)]
        w2_words_by_t = w2_w[:].rearrange("p (m t) -> p t m", t=PACK)
        nc.scalar.copy(w2_d0[:], w2_words_by_t[:, 0, :])
        nc.scalar.copy(w2_d123[:], w2_words_by_t[:, 1:, :])
        w2_ds0 = keep.tile([P, P], U8, name="w2_ds0", tag="lhs_scales", align_bytes=64)
        w2_ds = [w2_ds0[:]]
        w2_by_t = w2_s[:].rearrange("p (m t) -> p t m", t=PACK)
        xog_s = keep.tile([P, J], U8, name="xog_s", tag="rhs_scales", align_bytes=64)
        xog_w = keep.tile([P, J], U32, name="xog_w", tag="rhs_words", align_bytes=64)
        b_sb = [keep.tile([P, J], F32, name=f"b_sb{t}") for t in range(PACK)]

        def product_b(t, lo, hi):
            acc = psum.tile([P, J], F32, name="acc_b", tag="bank")
            nc.tensor.matmul_mx(
                out=acc[:, lo:hi], lhsT=w2_d[t].bitcast(FP4X4), lhsT_scale=w2_ds[t],
                rhs=xog_w[:, lo:hi].bitcast(FP8X4), rhs_scale=xog_s[:, lo:hi], start=True, stop=True,
            )
            return acc[:, lo:hi]

        for lo, hi in HEAD_PIECES:
            nc.vector.tensor_copy(xog_s[:, lo:hi], xo_s[:].indirect(list2[:, cols16(lo, hi)]))
            nc.vector.tensor_copy(xog_w[:, lo:hi], xo_w[:].indirect(list2[:, cols16(lo, hi)]))
            if lo == 0:
                nc.vector.tensor_copy(w2_ds[0], w2_by_t[:, 0, :])
            acc = product_b(0, lo, hi)
            if hi < J:
                nc.scalar.copy(b_sb[0][:, lo:hi], acc)
            else:
                nc.vector.tensor_copy(b_sb[0][:, lo:hi], acc)
            nc.scalar.activation(pv[0][:].indirect(list4[:, cols16(lo, hi)]), b_sb[0][:, lo:hi], COPY)

        w2_rest = keep.tile([P, LAST, P], U8, name="w2_rest", tag="table_scales", align_bytes=64)
        nc.vector.tensor_copy(w2_rest[:], w2_by_t[:, 1:, :])
        w2_ds.extend(w2_rest[:, t, :] for t in range(LAST))
        for t in range(1, PACK):
            nc.vector.tensor_copy(b_sb[t][:], product_b(t, 0, J))

        xt_s = zero_plane(T, "xt_s", "table_scales")
        load_scales(xt_s, xt_scales)
        w_s = w2_s
        load_scales(w_s, w_scales)
        xtg_s = keep.tile([P, J], U8, name="xtg_s", tag="rhs_scales", align_bytes=64)
        xtg_w = keep.tile([P, J], U16, name="xtg_w", tag="rhs_words", align_bytes=64)
        nc.vector.tensor_copy(xtg_w[:], xt_w[:].indirect(list1[:]))
        nc.vector.tensor_copy(xtg_s[:], xt_s[:].indirect(list1[:]))
        pw = [board("pw0", "slot_b", nc.vector), board("pw1", "table_scales", nc.vector)]
        w_d = keep.tile([P, PACK, P], U32, name="w_d", tag="lhs_words", align_bytes=64)
        nc.vector.tensor_copy(w_d[:].bitcast(I32), w_w[:].bitcast(I32).rearrange("p (m t) -> p t m", t=PACK))
        w_ds = keep.tile([P, PACK, P], U8, name="w_ds", tag="lhs_scales", align_bytes=64)
        nc.vector.tensor_copy(w_ds[:], w_s[:].rearrange("p (m t) -> p t m", t=PACK))
        a_sb = [[keep.tile([P, HALF], F32, name=f"a_sb{t}{h}") for h in range(2)] if t == LAST
                else keep.tile([P, J], F32, name=f"a_sb{t}") for t in range(PACK)]
        for t in range(PACK):
            acc = psum.tile([P, J], F32, name="acc_a", tag="bank")
            nc.tensor.matmul_mx(
                out=acc[:], lhsT=w_d[:, t, :].bitcast(FP8X4), lhsT_scale=w_ds[:, t, :],
                rhs=xtg_w[:].bitcast(FP4X4), rhs_scale=xtg_s[:], start=True, stop=True,
            )
            if t == LAST:
                for h in range(2):
                    nc.vector.tensor_copy(a_sb[t][h][:], acc[:, h * HALF : (h + 1) * HALF])
            else:
                nc.vector.tensor_copy(a_sb[t][:], acc[:])

        gate = [keep.tile([P, O], F32, name=f"gate{t}") for t in range(LAST)]
        value = [keep.tile([P, O], F32, name=f"value{t}") for t in range(PACK)]
        hid = [keep.tile([P, hi - lo, PACK], BF16, name=f"hid{lo}", align_bytes=64) for lo, hi in OUT_PIECES]

        def put_gate(t):
            nc.scalar.activation(pv[t % 2][:].indirect(list4[:]), b_sb[t][:], COPY)

        def put_value(t):
            nc.scalar.activation(pw[t % 2][:].indirect(list3[:]), a_sb[t][:], COPY)

        def get_gate(t, lo, hi, dst):
            nc.scalar.activation(
                dst, pv[t % 2][:].indirect(list6[:, cols16(lo, hi)]), SIGMOID,
                scale=sl_t[:, t : t + 1], bias=gf_t[:, t : t + 1],
            )

        def get_value(t, lo, hi):
            nc.scalar.activation(
                value[t][:, lo:hi], pw[t % 2][:].indirect(list5[:, cols16(lo, hi)]), COPY,
                scale=sa_t[:, t : t + 1],
            )

        def multiply(t, i, gates):
            lo, hi = OUT_PIECES[i]
            nc.vector.tensor_tensor(hid[i][:, :, t], value[t][:, lo:hi], gates, MULT)

        def finish(i):
            lo, hi = OUT_PIECES[i]
            width = hi - lo
            codes = keep.tile([P, width], U32, name=f"codes{i}", align_bytes=64)
            scales = keep.tile([P, width], U8, name=f"scales{i}", align_bytes=64)
            nc.vector.quantize_mx(
                out=codes[:].bitcast(FP8X4), scales=scales[:], in_=hid[i][:].rearrange("p o t -> p (o t)")
            )
            res = keep.tile([P, 2, width], F32, name=f"res{i}")
            split = hi == O
            acc = None
            for n in range(2):
                if n == 0 or split:
                    acc = psum.tile([P, 2, HALF], F32, name="acc_o", tag="bank")
                nc.tensor.matmul_mx(
                    out=acc[:, n, :width], lhsT=wb_w[:, n * P : (n + 1) * P].bitcast(FP4X4),
                    lhsT_scale=wb_s[:, n * P : (n + 1) * P],
                    rhs=codes[:].bitcast(FP8X4), rhs_scale=scales[:], start=True, stop=True,
                )
                if split and n == 0:
                    nc.vector.tensor_copy(res[:, n, :], acc[:, n, :width])
                elif split:
                    nc.scalar.copy(res[:, n, :], acc[:, n, :width])
            if not split:
                nc.scalar.copy(res[:], acc[:, :, :width])
            nc.sync.dma_start(out.rearrange("(n p) o -> p n o", p=P)[:, :, lo:hi], res[:])

        def value_and_products(t):
            get_value(t, 0, O)
            for i, (lo, hi) in enumerate(OUT_PIECES):
                multiply(t, i, gate[t][:, lo:hi])

        def put_last_value(h):
            nc.scalar.activation(
                pw[LAST % 2][:].indirect(list3[:, cols16(h * HALF, (h + 1) * HALF)]), a_sb[LAST][h][:], COPY
            )

        for t in range(1, PACK):
            put_gate(t)
            get_gate(t - 1, 0, O, gate[t - 1][:])
        put_value(0)
        put_value(1)
        value_and_products(0)
        value_and_products(1)
        put_value(2)
        put_last_value(0)
        value_and_products(2)
        put_last_value(1)
        for h in range(2):
            last_gate = keep.tile([P, HALF], F32, name="last_gate", tag=f"a_sb{LAST}{h}")
            get_gate(LAST, h * HALF, (h + 1) * HALF, last_gate[:])
            get_value(LAST, h * HALF, (h + 1) * HALF)
            for i, (lo, hi) in enumerate(OUT_PIECES):
                if lo // HALF == h:
                    multiply(LAST, i, last_gate[:, lo - h * HALF : hi - h * HALF])
            for i, (lo, hi) in enumerate(OUT_PIECES):
                if lo // HALF == h:
                    finish(i)
